import numpy as np
import ml_dtypes


def mxq(x, axis, fmt="e4m3"):
    dtype, down = {"e4m3": (ml_dtypes.float8_e4m3fn, 7), "e5m2": (ml_dtypes.float8_e5m2, 14)}[fmt]
    v = np.moveaxis(np.asarray(x, np.float32).astype(ml_dtypes.bfloat16).astype(np.float64), axis, -1)
    blocks = v.reshape(v.shape[:-1] + (-1, 32))
    amax = np.abs(blocks).max(-1, keepdims=True)
    byte = np.maximum(np.where(amax > 0, np.frexp(amax)[1] - 1 + 127, 0) - down, 1)
    scale = np.exp2(byte - 127.0)
    codes = (blocks / scale).astype(np.float32).astype(dtype).astype(np.float64)
    return np.moveaxis((codes * scale).reshape(v.shape), -1, axis)


WIDE = False


def mx_kscale(k):
    if not WIDE:
        return np.ones(k)
    levels = np.array([10, -10, 5, -5, 0])
    if k % 512:
        return np.exp2(np.random.permutation(np.resize(levels, k // 32))).repeat(32)
    a = np.empty((k // 512, 16))
    for p in range(k // 512):
        a[p, :8] = np.random.permutation(np.resize(levels, 8))
        for g in range(8):
            far = levels[np.abs(levels - a[p, g]) >= 10]
            a[p, g + 8] = far[np.random.randint(len(far))]
    return np.exp2(a.ravel()).repeat(32)


def f64(x):
    return np.asarray(x).astype(np.float64)


def striped(idx):
    return np.tile(idx.reshape(-1, 16).T, (8, 1)).astype(np.uint16)


def unstriped(offs):
    return offs[:16].T.reshape(-1).astype(np.int64)


def striped8(idx):
    return np.concatenate([x.reshape(-1, 16).T for x in idx]).astype(np.uint16)


def runs(offs, k):
    lists = np.stack([offs[16 * r : 16 * r + 16].T.reshape(-1) for r in range(8)]).astype(np.int64)
    return lists[np.arange(k) % 512 // 64]


def pack_weight(w):
    k, n = w.shape
    w = f64(np.asarray(w, np.float32).astype(ml_dtypes.bfloat16)).reshape(k // 32, 32, n)
    amax = np.abs(w).max(1)
    byte = np.clip(np.where(amax > 0, np.frexp(amax)[1] - 1 + 127 - 7, 1), 1, 254)
    scaled = (w * np.exp2(127.0 - byte)[:, None, :]).reshape(k, n).astype(np.float32)
    words = np.ascontiguousarray(scaled.reshape(k // 512, 128, 4, n).transpose(0, 1, 3, 2)).astype(ml_dtypes.float8_e4m3fn).view(np.uint8)
    return words, np.ascontiguousarray(byte.astype(np.uint8).reshape(k // 512, 16, n))


def unpack_weight(words, scales):
    g, p, n, _ = words.shape
    vals = np.ascontiguousarray(words).view(ml_dtypes.float8_e4m3fn).astype(np.float64) * np.repeat(np.exp2(scales.astype(np.float64) - 127.0), 8, axis=1)[..., None]
    return vals.transpose(0, 1, 3, 2).reshape(g * 512, n)


def sigmoid(v):
    return 1.0 / (1.0 + np.exp(-np.maximum(v, -700.0)))

def planes(y):
    n, m = y.shape
    v = y.astype(np.float32).astype(ml_dtypes.bfloat16).astype(np.float64).reshape(n // 32, 32, m)
    top = np.abs(v).max(1)
    byte = np.clip(np.where(top > 0, np.frexp(top)[1] - 1 + 127 - 7, 1), 1, 254)
    codes = (v * np.exp2(127.0 - byte)[:, None, :]).reshape(n, m).astype(np.float32).astype(ml_dtypes.float8_e4m3fn).view(np.uint8)
    words = codes.reshape(n // 512, 128, 4, m).transpose(0, 1, 3, 2)
    return np.ascontiguousarray(words), np.ascontiguousarray(byte.astype(np.uint8).reshape(n // 512, 16, m))


K, T, S, N, H = 512, 2048, 512, 512, 512


def setup_inputs():
    n = np.random.standard_normal
    s = mx_kscale(K)[:, None]
    u = mx_kscale(H)
    packed_xT = pack_weight(n((K, T)) * s)
    packed_w1 = pack_weight(n((K, H)) / np.sqrt(K) / s)
    packed_w2 = pack_weight(n((K, H)) / np.sqrt(K) / s)
    packed_w3 = pack_weight(n((K, H)) / np.sqrt(K) / s)
    packed_w4 = pack_weight(n((H, N)) / np.sqrt(H) / u[:, None])
    return {
        "x_words": packed_xT[0],
        "x_scales": packed_xT[1],
        "w1_words": packed_w1[0],
        "w1_scales": packed_w1[1],
        "w2_words": packed_w2[0],
        "w2_scales": packed_w2[1],
        "w3_words": packed_w3[0],
        "w3_scales": packed_w3[1],
        "sl": np.random.uniform(1.0, 2.0, (H, 1)).astype(np.float32),
        "th": (0.5 * n((H, 1))).astype(np.float32),
        "gn": (np.random.uniform(0.5, 1.5, (H, 1)) * u[:, None]).astype(np.float32),
        "w4_words": packed_w4[0],
        "w4_scales": packed_w4[1],
        "offs": striped(np.random.permutation(T)[:S]),
        "two": striped(np.random.permutation(T)[:S]),
        "three": striped(np.random.permutation(T)[:S]),
        "n1": striped(np.random.permutation(S)),
        "n2": striped(np.random.permutation(S)),
        "n3": striped8(np.stack([np.random.permutation(S) for _ in range(8)])),
        "n4": striped8(np.stack([np.random.permutation(S) for _ in range(8)])),
        "n5": striped8(np.stack([np.random.permutation(S) for _ in range(8)])),
        "n6": striped8(np.stack([np.random.permutation(S) for _ in range(8)])),
        "n7": striped8(np.stack([np.random.permutation(S) for _ in range(8)])),
        "n8": striped8(np.stack([np.random.permutation(S) for _ in range(8)])),
    }


def reference(x_words, x_scales, w1_words, w1_scales, w2_words, w2_scales, w3_words, w3_scales, sl, th, gn, w4_words, w4_scales, offs, two, three, n1, n2, n3, n4, n5, n6, n7, n8):
    xq = unpack_weight(x_words, x_scales)[:, unstriped(offs)]
    y = unpack_weight(w1_words, w1_scales).T @ xq
    x_two = unpack_weight(x_words, x_scales)[:, unstriped(two)]
    d = unpack_weight(w2_words, w2_scales).T @ x_two
    m1 = y + (sigmoid(d[:, unstriped(n2)] - d)) * (y[:, unstriped(n1)] - y)
    x_three = unpack_weight(x_words, x_scales)[:, unstriped(three)]
    b = unpack_weight(w3_words, w3_scales).T @ x_three
    sg = sigmoid(f64(sl) * (b[np.arange(H)[:, None], runs(n3, H)] - f64(th)))
    z = f64(gn) * (m1 * sg - (0.5 * (m1[np.arange(H)[:, None], runs(n4, H)])))
    h = unpack_weight(w4_words, w4_scales).T @ mxq(z, 0, "e4m3")
    out_0 = 0.75 * ((h[np.arange(N)[:, None], runs(n5, N)]) * (h[np.arange(N)[:, None], runs(n6, N)]) - ((h[np.arange(N)[:, None], runs(n7, N)]) * (h[np.arange(N)[:, None], runs(n8, N)])))
    return (out_0,) + planes(out_0)

@@ -1,0 +1,256 @@
+from contextlib import ExitStack
+
+import concourse.mybir as mybir
+
+F32 = mybir.dt.float32
+BF16 = mybir.dt.bfloat16
+I32 = mybir.dt.int32
+U32 = mybir.dt.uint32
+U16 = mybir.dt.uint16
+U8 = mybir.dt.uint8
+FP8X4 = mybir.dt.float8_e4m3fn_x4
+MULT = mybir.AluOpType.mult
+ADD = mybir.AluOpType.add
+SUB = mybir.AluOpType.subtract
+COPY = mybir.ActivationFunctionType.Copy
+SIGMOID = mybir.ActivationFunctionType.Sigmoid
+
+P = 128
+T = 2048
+S = 512
+PACK = 4
+HALF = S // 2
+FLOPS = 4 * 2 * 512 * 512 * 512
+
+
+def tile_picked_triopullbgxbdet_none_po_kernel(
+    tc, x_words, x_scales, w1_words, w1_scales, w2_words, w2_scales, w3_words, w3_scales, sl, th, gn,
+    w4_words, w4_scales, offs, two, three, n1, n2, n3, n4, n5, n6, n7, n8, out_0, out_1, out_2,
+):
+    nc = tc.nc
+    with ExitStack() as ctx:
+        keep = ctx.enter_context(tc.tile_pool(name="keep", bufs=1))
+        psum = ctx.enter_context(tc.psum_pool(name="psum", bufs=1))
+
+        def sb(name, shape, dtype):
+            return keep.tile(shape, dtype, name=name, align_bytes=64)
+
+        def bank(number, name, width):
+            return psum.tile([P, width], F32, name=name, tag="bank%d" % number)
+
+        lists = {}
+
+        def load_list(name, ap):
+            lists[name] = sb("list_" + name, [P, S // 16], U16)
+            nc.sync.dma_start(lists[name][:], ap)
+
+        def offsets(name, h):
+            return lists[name][:, h * HALF // 16 : (h + 1) * HALF // 16]
+
+        def half(h):
+            return slice(h * HALF, (h + 1) * HALF)
+
+        def load_words(queue, name, ap, width):
+            words = sb(name, [P, width], U32)
+            queue.dma_start(words[:].bitcast(I32), ap[0].rearrange("p n t -> p (n t)").bitcast(I32))
+            return words
+
+        def load_scales(queue, name, ap, width):
+            plane = sb(name, [P, width], U8)
+            for q in range(4):
+                rows = ap[0, 4 * q : 4 * q + 4, :].bitcast(I32)
+                queue.dma_start(plane[32 * q : 32 * q + 32, :].bitcast(I32), rows.partition_broadcast(8))
+            return plane
+
+        def load_column(queue, name, ap):
+            column = sb(name, [P, PACK], F32)
+            queue.dma_start(column[:], ap.rearrange("(p t) o -> p (t o)", t=PACK))
+            return column
+
+        def deal(copy, name, raw, dtype, run):
+            dealt = sb(name, [P, S], dtype)
+            copy(
+                dealt[:].rearrange("p (t c i) -> p c t i", t=PACK, i=run),
+                raw[:].rearrange("p (c i t) -> p c t i", t=PACK, i=run),
+            )
+            return dealt
+
+        load_list("two", two)
+        xs = load_scales(nc.sync, "xs", x_scales, T)
+        load_list("offs", offs)
+        xw = load_words(nc.sync, "xw", x_words, T)
+        raw_s2 = load_scales(nc.sync, "raw_s2", w2_scales, S)
+        raw_w2 = load_words(nc.sync, "raw_w2", w2_words, S)
+        load_list("three", three)
+        load_list("n2", n2)
+        raw_w1 = load_words(nc.sync, "raw_w1", w1_words, S)
+        raw_s1 = load_scales(nc.sync, "raw_s1", w1_scales, S)
+        gain = load_column(nc.sync, "gain", gn)
+        load_list("n1", n1)
+        raw_w3 = load_words(nc.sync, "raw_w3", w3_words, S)
+        raw_s3 = load_scales(nc.sync, "raw_s3", w3_scales, S)
+        slope = load_column(nc.sync, "slope", sl)
+        thresh = load_column(nc.sync, "thresh", th)
+        load_list("n3", n3)
+        load_list("n4", n4)
+        raw_w4 = load_words(nc.sync, "raw_w4", w4_words, S)
+        raw_s4 = load_scales(nc.sync, "raw_s4", w4_scales, S)
+        for name, ap in (("n5", n5), ("n6", n6), ("n7", n7), ("n8", n8)):
+            load_list(name, ap)
+
+        def pick_words(name):
+            words = sb("pw_" + name, [P, S], U32)
+            nc.vector.tensor_copy(words[:], xw[:].indirect(lists[name][:]))
+            return words
+
+        def pick_scales(name):
+            scales = sb("ps_" + name, [P, S], U8)
+            nc.vector.tensor_copy(scales[:], xs[:].indirect(lists[name][:]))
+            return scales
+
+        def product(acc, w_words, w_plane, first, t, words, scales):
+            cols = slice(t * P, (t + 1) * P)
+            nc.tensor.matmul_mx(
+                out=acc[:], lhsT=w_words[:, cols].bitcast(FP8X4), lhsT_scale=w_plane[first:P, cols],
+                rhs=words.bitcast(FP8X4), rhs_scale=scales, start=True, stop=True,
+            )
+
+        bias = sb("bias", [P, PACK], F32)
+        gate = {}
+
+        def gate_of(t, number, copy):
+            acc = bank(number, "b_acc%d" % t, S)
+            product(acc, w3, s3, 0, t, xw3[:], xs3[:])
+            b = sb("b%d" % t, [P, S], F32)
+            copy(b[:], acc[:])
+            gate[t] = sb("sg%d" % t, [P, S], F32)
+            for h in range(2):
+                nc.scalar.activation(
+                    gate[t][:, half(h)], b[:].indirect(offsets("n3", h)), SIGMOID,
+                    bias=bias[:, t : t + 1], scale=slope[:, t : t + 1],
+                )
+
+        xs2 = pick_scales("two")
+        xs1 = pick_scales("offs")
+        xw2 = pick_words("two")
+        s2 = deal(nc.gpsimd.tensor_copy, "s2", raw_s2, U8, 16)
+        w2 = deal(nc.scalar.copy, "w2", raw_w2, U32, 4)
+        xw1 = pick_words("offs")
+        xs3 = pick_scales("three")
+        xw3 = pick_words("three")
+        w1 = deal(nc.gpsimd.tensor_copy, "w1", raw_w1, U32, 4)
+        s1 = deal(nc.gpsimd.tensor_copy, "s1", raw_s1, U8, 16)
+        w3 = deal(nc.gpsimd.tensor_copy, "w3", raw_w3, U32, 4)
+        s3 = deal(nc.gpsimd.tensor_copy, "s3", raw_s3, U8, 16)
+        w4 = deal(nc.gpsimd.tensor_copy, "w4", raw_w4, U32, 4)
+        s4 = deal(nc.gpsimd.tensor_copy, "s4", raw_s4, U8, 16)
+        nc.vector.scalar_tensor_tensor(bias[:], slope[:], -1.0, thresh[:], MULT, MULT)
+
+        mix = {}
+        y = {}
+        a = sb("a", [P, PACK, S], F32)
+        pulled = [sb("pulled%d" % h, [P, PACK, HALF], F32) for h in range(2)]
+
+        def front(t):
+            d_acc = bank(t, "d_acc%d" % t, S)
+            product(d_acc, w2, s2, 0, t, xw2[:], xs2[:])
+            d = sb("d%d" % t, [P, S], F32)
+            nc.scalar.copy(d[:], d_acc[:])
+            diff = sb("diff%d" % t, [P, S], F32)
+            for h in range(2):
+                nc.scalar.activation(diff[:, half(h)], d[:].indirect(offsets("n2", h)), COPY)
+            nc.vector.tensor_tensor(diff[:], diff[:], d_acc[:], SUB)
+            y_acc = bank(4 + t, "y_acc%d" % t, S)
+            product(y_acc, w1, s1, 0, t, xw1[:], xs1[:])
+            y[t] = sb("y%d" % t, [P, S], F32)
+            nc.vector.tensor_scalar(y[t][:], y_acc[:], gain[:, t : t + 1], None, MULT)
+            mix[t] = sb("mix%d" % t, [P, S], F32)
+            nc.scalar.activation(mix[t][:], diff[:], SIGMOID)
+
+        def blend(t):
+            u = sb("u%d" % t, [P, S], F32)
+            for h in range(2):
+                nc.vector.tensor_tensor(u[:, half(h)], y[t][:].indirect(offsets("n1", h)), mix[t][:, half(h)], MULT)
+            v = sb("v%d" % t, [P, S], F32)
+            nc.vector.scalar_tensor_tensor(v[:], mix[t][:], 1.0, y[t][:], SUB, MULT)
+            m[t] = sb("m%d" % t, [P, S], F32)
+            nc.vector.tensor_tensor(m[t][:], u[:], v[:], SUB)
+
+        def pull(t):
+            for h in range(2):
+                nc.scalar.activation(pulled[h][:, t, :], m[t][:].indirect(offsets("n4", h)), COPY, scale=-0.5)
+            nc.vector.tensor_tensor(a[:, t, :], m[t][:], gate[t][:], MULT)
+
+        m = {}
+        front(0)
+        front(1)
+        front(2)
+        front(3)
+        blend(0)
+        gate_of(0, 0, nc.scalar.copy)
+        blend(1)
+        gate_of(1, 1, nc.scalar.copy)
+        pull(0)
+        blend(2)
+        gate_of(2, 2, nc.vector.tensor_copy)
+        pull(1)
+        blend(3)
+        gate_of(3, 3, nc.vector.tensor_copy)
+        pull(2)
+        pull(3)
+
+        hs = [sb("h%d" % t, [P, S], F32) for t in range(PACK)]
+        for k, (c0, c1) in enumerate(((0,128),(128,256),(256,384),(384,512))):
+            h, w = c0 // HALF, c1 - c0
+            z = keep.tile([P, w * PACK], BF16, name="z%d" % k, align_bytes=64)
+            nc.vector.tensor_tensor(
+                z[:].rearrange("p (c i t) -> p c t i", t=PACK, i=4),
+                a[:, :, c0:c1].rearrange("p t (c i) -> p c t i", i=4),
+                pulled[h][:, :, c0 - h * HALF : c1 - h * HALF].rearrange("p t (c i) -> p c t i", i=4),
+                ADD,
+            )
+            zw = sb("zw%d" % k, [P, w], U32)
+            zs = sb("zs%d" % k, [P, w], U8)
+            nc.vector.quantize_mx(zw[:].bitcast(FP8X4), zs[:], z[:])
+            for t in range(PACK):
+                h_acc = bank((PACK * k + t) % 8, "h_acc%d_%d" % (k, t), w)
+                product(h_acc, w4, s4, 0, t, zw[:], zs[:])
+                if k == 3 and t % 2 == 1:
+                    nc.vector.tensor_copy(hs[t][:, c0:c1], h_acc[:])
+                else:
+                    nc.scalar.copy(hs[t][:, c0:c1], h_acc[:])
+
+        out_rows = out_0.rearrange("(p t) n -> p t n", t=PACK)
+        out_words = out_1[0].rearrange("p n t -> p (n t)").bitcast(I32)
+        o_scales = sb("o_scales", [P, S], U8)
+        for h in range(2):
+            o = sb("o%d" % h, [P, PACK, HALF], F32)
+            for t in range(PACK):
+                terms = []
+                for first, second, factor in (("n5", "n6", 0.75), ("n7", "n8", -0.75)):
+                    g = sb("g%s_%d_%d" % (first, t, h), [P, HALF], F32)
+                    nc.scalar.activation(g[:], hs[t][:].indirect(offsets(first, h)), COPY, scale=factor)
+                    term = sb("term%s_%d_%d" % (first, t, h), [P, HALF], F32)
+                    if first == "n7" and t == 2:
+                        g2 = sb("gg%s_%d_%d" % (first, t, h), [P, HALF], F32)
+                        nc.scalar.activation(g2[:], hs[t][:].indirect(offsets(second, h)), COPY)
+                        nc.vector.tensor_tensor(term[:], g2[:], g[:], MULT)
+                    else:
+                        nc.vector.tensor_tensor(term[:], hs[t][:].indirect(offsets(second, h)), g[:], MULT)
+                    terms.append(term)
+                nc.vector.tensor_tensor(o[:, t, :], terms[0][:], terms[1][:], ADD)
+                nc.sync.dma_start(out_rows[:, t, half(h)], o[:, t, :])
+            ob = sb("ob%d" % h, [P, HALF * PACK], BF16)
+            cast = nc.scalar.copy if h == 0 else nc.vector.tensor_copy
+            cast(
+                ob[:].rearrange("p (c i t) -> p c t i", t=PACK, i=4),
+                o[:].rearrange("p t (c i) -> p c t i", i=4),
+            )
+            ow = sb("ow%d" % h, [P, HALF], U32)
+            nc.vector.quantize_mx(ow[:].bitcast(FP8X4), o_scales[:, half(h)], ob[:])
+            nc.sync.dma_start(out_words[:, half(h)], ow[:].bitcast(I32))
+        for q in range(4):
+            queue = nc.sync if q % 2 == 0 else nc.scalar
+            queue.dma_start(
+                out_2[0, 4 * q : 4 * q + 4, :].bitcast(I32), o_scales[32 * q : 32 * q + 4, :].bitcast(I32)
+            )

@@ -62,6 +62,16 @@ def tile_picked_triopullbgxbdet_none_po_kernel(
                 queue.dma_start(plane[32 * q : 32 * q + 32, :].bitcast(I32), rows.partition_broadcast(8))
             return plane
 
+        def zeroed_plane(name):
+            plane = sb(name, [P, S], U8)
+            nc.vector.memset(plane[:].bitcast(I32), 0)
+            return plane
+
+        def load_rows(plane, first, ap):
+            for q in range(4):
+                rows = slice(32 * q + first, 32 * q + first + 4)
+                nc.sync.dma_start(plane[rows, :].bitcast(I32), ap[0, 4 * q : 4 * q + 4, :].bitcast(I32))
+
         def load_column(queue, name, ap):
             column = sb(name, [P, PACK], F32)
             queue.dma_start(column[:], ap.rearrange("(p t) o -> p (t o)", t=PACK))
@@ -75,31 +85,36 @@ def tile_picked_triopullbgxbdet_none_po_kernel(
             )
             return dealt
 
+        raw_s13 = zeroed_plane("raw_s13")
+        raw_s2 = zeroed_plane("raw_s2")
+        raw_s4 = zeroed_plane("raw_s4")
         load_list("two", two)
         xs = load_scales(nc.sync, "xs", x_scales, T)
-        load_list("offs", offs)
-        xw = load_words(nc.sync, "xw", x_words, T)
-        raw_s2 = load_scales(nc.sync, "raw_s2", w2_scales, S)
-        raw_w2 = load_words(nc.sync, "raw_w2", w2_words, S)
         load_list("three", three)
-        load_list("n2", n2)
+        xw = load_words(nc.sync, "xw", x_words, T)
+        load_rows(raw_s2, 0, w2_scales)
+        raw_w2 = load_words(nc.sync, "raw_w2", w2_words, S)
         raw_w1 = load_words(nc.sync, "raw_w1", w1_words, S)
-        raw_s1 = load_scales(nc.sync, "raw_s1", w1_scales, S)
+        load_list("offs", offs)
+        raw_w3 = load_words(nc.sync, "raw_w3", w3_words, S)
+        load_rows(raw_s13, 0, w1_scales)
+        load_rows(raw_s13, 4, w3_scales)
+        load_list("n2", n2)
         gain = load_column(nc.sync, "gain", gn)
         load_list("n1", n1)
-        raw_w3 = load_words(nc.sync, "raw_w3", w3_words, S)
-        raw_s3 = load_scales(nc.sync, "raw_s3", w3_scales, S)
         slope = load_column(nc.sync, "slope", sl)
         thresh = load_column(nc.sync, "thresh", th)
         load_list("n3", n3)
         load_list("n4", n4)
         raw_w4 = load_words(nc.sync, "raw_w4", w4_words, S)
-        raw_s4 = load_scales(nc.sync, "raw_s4", w4_scales, S)
-        for name, ap in (("n5", n5), ("n6", n6), ("n7", n7), ("n8", n8)):
-            load_list(name, ap)
+        load_rows(raw_s4, 0, w4_scales)
+        load_list("n5", n5)
+        load_list("n6", n6)
+        load_list("n7", n7)
+        load_list("n8", n8)
 
-        def pick_words(name):
-            words = sb("pw_" + name, [P, S], U32)
+        def pick_words(name, tag):
+            words = keep.tile([P, S], U32, name="pw_" + name, tag=tag, align_bytes=64)
             nc.vector.tensor_copy(words[:], xw[:].indirect(lists[name][:]))
             return words
 
@@ -120,7 +135,7 @@ def tile_picked_triopullbgxbdet_none_po_kernel(
 
         def gate_of(t, number, copy):
             acc = bank(number, "b_acc%d" % t, S)
-            product(acc, w3, s3, 0, t, xw3[:], xs3[:])
+            product(acc, w3, s13, 4, t, xw3[:], xs3[:])
             b = sb("b%d" % t, [P, S], F32)
             copy(b[:], acc[:])
             gate[t] = sb("sg%d" % t, [P, S], F32)
@@ -131,19 +146,21 @@ def tile_picked_triopullbgxbdet_none_po_kernel(
                 )
 
         xs2 = pick_scales("two")
-        xs1 = pick_scales("offs")
-        xw2 = pick_words("two")
-        s2 = deal(nc.gpsimd.tensor_copy, "s2", raw_s2, U8, 16)
-        w2 = deal(nc.scalar.copy, "w2", raw_w2, U32, 4)
-        xw1 = pick_words("offs")
         xs3 = pick_scales("three")
-        xw3 = pick_words("three")
-        w1 = deal(nc.gpsimd.tensor_copy, "w1", raw_w1, U32, 4)
-        s1 = deal(nc.gpsimd.tensor_copy, "s1", raw_s1, U8, 16)
-        w3 = deal(nc.gpsimd.tensor_copy, "w3", raw_w3, U32, 4)
-        s3 = deal(nc.gpsimd.tensor_copy, "s3", raw_s3, U8, 16)
-        w4 = deal(nc.gpsimd.tensor_copy, "w4", raw_w4, U32, 4)
-        s4 = deal(nc.gpsimd.tensor_copy, "s4", raw_s4, U8, 16)
+        xw2 = pick_words("two", "pw_a")
+        s2 = deal(nc.vector.tensor_copy, "s2", raw_s2, U8, 16)
+        w2 = deal(nc.scalar.copy, "w2", raw_w2, U32, 4)
+        d_accs = [bank(t, "d_acc%d" % t, S) for t in range(PACK)]
+        for t in range(PACK):
+            product(d_accs[t], w2, s2, 0, t, xw2[:], xs2[:])
+        xs1 = pick_scales("offs")
+        xw1 = pick_words("offs", "pw_b")
+        w1 = deal(nc.scalar.copy, "w1", raw_w1, U32, 4)
+        w3 = deal(nc.scalar.copy, "w3", raw_w3, U32, 4)
+        s13 = deal(nc.vector.tensor_copy, "s13", raw_s13, U8, 16)
+        xw3 = pick_words("three", "pw_a")
+        w4 = deal(nc.scalar.copy, "w4", raw_w4, U32, 4)
+        s4 = deal(nc.vector.tensor_copy, "s4", raw_s4, U8, 16)
         nc.vector.scalar_tensor_tensor(bias[:], slope[:], -1.0, thresh[:], MULT, MULT)
 
         mix = {}
@@ -152,18 +169,21 @@ def tile_picked_triopullbgxbdet_none_po_kernel(
         pulled = [sb("pulled%d" % h, [P, PACK, HALF], F32) for h in range(2)]
 
         def front(t):
-            d_acc = bank(t, "d_acc%d" % t, S)
-            product(d_acc, w2, s2, 0, t, xw2[:], xs2[:])
+            d_acc = d_accs[t]
             d = sb("d%d" % t, [P, S], F32)
             nc.scalar.copy(d[:], d_acc[:])
+            twin = sb("twin%d" % t, [P, S], F32)
+            nc.scalar.dma_start(twin[:], d[:])
             diff = sb("diff%d" % t, [P, S], F32)
             for h in range(2):
-                nc.scalar.activation(diff[:, half(h)], d[:].indirect(offsets("n2", h)), COPY)
-            nc.vector.tensor_tensor(diff[:], diff[:], d_acc[:], SUB)
+                nc.vector.tensor_tensor(diff[:, half(h)], d[:].indirect(offsets("n2", h)), twin[:, half(h)], SUB)
             y_acc = bank(4 + t, "y_acc%d" % t, S)
-            product(y_acc, w1, s1, 0, t, xw1[:], xs1[:])
+            product(y_acc, w1, s13, 0, t, xw1[:], xs1[:])
             y[t] = sb("y%d" % t, [P, S], F32)
-            nc.vector.tensor_scalar(y[t][:], y_acc[:], gain[:, t : t + 1], None, MULT)
+            if t == 0:
+                nc.vector.tensor_scalar(y[t][:], y_acc[:], gain[:, t : t + 1], None, MULT)
+            else:
+                nc.scalar.activation(y[t][:], y_acc[:], COPY, scale=gain[:, t : t + 1])
             mix[t] = sb("mix%d" % t, [P, S], F32)
             nc.scalar.activation(mix[t][:], diff[:], SIGMOID)
 
@@ -186,16 +206,16 @@ def tile_picked_triopullbgxbdet_none_po_kernel(
         front(1)
         front(2)
         front(3)
-        blend(0)
         gate_of(0, 0, nc.scalar.copy)
-        blend(1)
         gate_of(1, 1, nc.scalar.copy)
+        blend(0)
+        gate_of(2, 2, nc.scalar.copy)
+        blend(1)
+        gate_of(3, 3, nc.scalar.copy)
         pull(0)
         blend(2)
-        gate_of(2, 2, nc.vector.tensor_copy)
         pull(1)
         blend(3)
-        gate_of(3, 3, nc.vector.tensor_copy)
         pull(2)
         pull(3)
 
@@ -223,32 +243,38 @@ def tile_picked_triopullbgxbdet_none_po_kernel(
         out_rows = out_0.rearrange("(p t) n -> p t n", t=PACK)
         out_words = out_1[0].rearrange("p n t -> p (n t)").bitcast(I32)
         o_scales = sb("o_scales", [P, S], U8)
-        for h in range(2):
-            o = sb("o%d" % h, [P, PACK, HALF], F32)
+        for k, (c0, c1) in enumerate(((0,256),(256,512))):
+            w = c1 - c0
+            o = sb("o%d" % k, [P, PACK, w], F32)
             for t in range(PACK):
                 terms = []
                 for first, second, factor in (("n5", "n6", 0.75), ("n7", "n8", -0.75)):
-                    g = sb("g%s_%d_%d" % (first, t, h), [P, HALF], F32)
-                    nc.scalar.activation(g[:], hs[t][:].indirect(offsets(first, h)), COPY, scale=factor)
-                    term = sb("term%s_%d_%d" % (first, t, h), [P, HALF], F32)
+                    g = sb("g%s_%d_%d" % (first, t, k), [P, w], F32)
+                    nc.scalar.activation(g[:], hs[t][:].indirect(lists[first][:, c0 // 16 : c1 // 16]), COPY, scale=factor)
+                    term = sb("term%s_%d_%d" % (first, t, k), [P, w], F32)
+                    window = hs[t][:].indirect(lists[second][:, c0 // 16 : c1 // 16])
                     if first == "n7" and t == 2:
-                        g2 = sb("gg%s_%d_%d" % (first, t, h), [P, HALF], F32)
-                        nc.scalar.activation(g2[:], hs[t][:].indirect(offsets(second, h)), COPY)
+                        g2 = sb("gg%s_%d_%d" % (first, t, k), [P, w], F32)
+                        nc.scalar.activation(g2[:], window, COPY)
+                        nc.vector.tensor_tensor(term[:], g2[:], g[:], MULT)
+                    elif False:
+                        g2 = sb("gg%s_%d_%d" % (first, t, k), [P, w], F32)
+                        nc.vector.tensor_copy(g2[:], window)
                         nc.vector.tensor_tensor(term[:], g2[:], g[:], MULT)
                     else:
-                        nc.vector.tensor_tensor(term[:], hs[t][:].indirect(offsets(second, h)), g[:], MULT)
+                        nc.vector.tensor_tensor(term[:], window, g[:], MULT)
                     terms.append(term)
                 nc.vector.tensor_tensor(o[:, t, :], terms[0][:], terms[1][:], ADD)
-                nc.sync.dma_start(out_rows[:, t, half(h)], o[:, t, :])
-            ob = sb("ob%d" % h, [P, HALF * PACK], BF16)
-            cast = nc.scalar.copy if h == 0 else nc.vector.tensor_copy
+                nc.sync.dma_start(out_rows[:, t, c0:c1], o[:, t, :])
+            ob = sb("ob%d" % k, [P, w * PACK], BF16)
+            cast = nc.scalar.copy if k == 0 else nc.vector.tensor_copy
             cast(
                 ob[:].rearrange("p (c i t) -> p c t i", t=PACK, i=4),
                 o[:].rearrange("p t (c i) -> p c t i", i=4),
             )
-            ow = sb("ow%d" % h, [P, HALF], U32)
-            nc.vector.quantize_mx(ow[:].bitcast(FP8X4), o_scales[:, half(h)], ob[:])
-            nc.sync.dma_start(out_words[:, half(h)], ow[:].bitcast(I32))
+            ow = sb("ow%d" % k, [P, w], U32)
+            nc.vector.quantize_mx(ow[:].bitcast(FP8X4), o_scales[:, c0:c1], ob[:])
+            nc.sync.dma_start(out_words[:, c0:c1], ow[:].bitcast(I32))
         for q in range(4):
             queue = nc.sync if q % 2 == 0 else nc.scalar
             queue.dma_start(

@@ -63,7 +63,7 @@ def tile_picked_triopullbgxbdet_none_po_kernel(
             return plane
 
         def zeroed_plane(name):
-            plane = sb(name, [P, S], U8)
+            plane = keep.tile([P, S], U8, name=name, tag=name, align_bytes=64)
             nc.vector.memset(plane[:].bitcast(I32), 0)
             return plane
 
@@ -90,21 +90,21 @@ def tile_picked_triopullbgxbdet_none_po_kernel(
         raw_s4 = zeroed_plane("raw_s4")
         load_list("two", two)
         xs = load_scales(nc.sync, "xs", x_scales, T)
-        load_list("three", three)
+        load_list("offs", offs)
         xw = load_words(nc.sync, "xw", x_words, T)
         load_rows(raw_s2, 0, w2_scales)
         raw_w2 = load_words(nc.sync, "raw_w2", w2_words, S)
-        raw_w1 = load_words(nc.sync, "raw_w1", w1_words, S)
-        load_list("offs", offs)
+        load_list("three", three)
         raw_w3 = load_words(nc.sync, "raw_w3", w3_words, S)
         load_rows(raw_s13, 0, w1_scales)
         load_rows(raw_s13, 4, w3_scales)
-        load_list("n2", n2)
+        raw_w1 = load_words(nc.sync, "raw_w1", w1_words, S)
         gain = load_column(nc.sync, "gain", gn)
-        load_list("n1", n1)
+        load_list("n2", n2)
         slope = load_column(nc.sync, "slope", sl)
         thresh = load_column(nc.sync, "thresh", th)
         load_list("n3", n3)
+        load_list("n1", n1)
         load_list("n4", n4)
         raw_w4 = load_words(nc.sync, "raw_w4", w4_words, S)
         load_rows(raw_s4, 0, w4_scales)
@@ -146,46 +146,57 @@ def tile_picked_triopullbgxbdet_none_po_kernel(
                 )
 
         xs2 = pick_scales("two")
-        xs3 = pick_scales("three")
+        xs1 = pick_scales("offs")
         xw2 = pick_words("two", "pw_a")
         s2 = deal(nc.vector.tensor_copy, "s2", raw_s2, U8, 16)
         w2 = deal(nc.scalar.copy, "w2", raw_w2, U32, 4)
         d_accs = [bank(t, "d_acc%d" % t, S) for t in range(PACK)]
         for t in range(PACK):
             product(d_accs[t], w2, s2, 0, t, xw2[:], xs2[:])
-        xs1 = pick_scales("offs")
-        xw1 = pick_words("offs", "pw_b")
-        w1 = deal(nc.scalar.copy, "w1", raw_w1, U32, 4)
+        xs3 = pick_scales("three")
+        xw3 = pick_words("three", "pw_b")
         w3 = deal(nc.scalar.copy, "w3", raw_w3, U32, 4)
         s13 = deal(nc.vector.tensor_copy, "s13", raw_s13, U8, 16)
-        xw3 = pick_words("three", "pw_a")
+        nc.vector.scalar_tensor_tensor(bias[:], slope[:], -1.0, thresh[:], MULT, MULT)
+        xw1 = pick_words("offs", "raw_s13")
+        w1 = deal(nc.scalar.copy, "w1", raw_w1, U32, 4)
         w4 = deal(nc.scalar.copy, "w4", raw_w4, U32, 4)
         s4 = deal(nc.vector.tensor_copy, "s4", raw_s4, U8, 16)
-        nc.vector.scalar_tensor_tensor(bias[:], slope[:], -1.0, thresh[:], MULT, MULT)
 
         mix = {}
         y = {}
         a = sb("a", [P, PACK, S], F32)
         pulled = [sb("pulled%d" % h, [P, PACK, HALF], F32) for h in range(2)]
 
-        def front(t):
-            d_acc = d_accs[t]
-            d = sb("d%d" % t, [P, S], F32)
-            nc.scalar.copy(d[:], d_acc[:])
-            twin = sb("twin%d" % t, [P, S], F32)
-            nc.scalar.dma_start(twin[:], d[:])
-            diff = sb("diff%d" % t, [P, S], F32)
-            for h in range(2):
-                nc.vector.tensor_tensor(diff[:, half(h)], d[:].indirect(offsets("n2", h)), twin[:, half(h)], SUB)
-            y_acc = bank(4 + t, "y_acc%d" % t, S)
+        def spread(t):
+            d[t] = sb("d%d" % t, [P, S], F32)
+            nc.scalar.copy(d[t][:], d_accs[t][:])
+            if True:
+                twin[t] = sb("twin%d" % t, [P, S], F32)
+                nc.scalar.dma_start(twin[t][:], d[t][:])
+
+        def differ(t):
+            diff[t] = sb("diff%d" % t, [P, S], F32)
+            if True:
+                for h in range(2):
+                    nc.vector.tensor_tensor(diff[t][:, half(h)], d[t][:].indirect(offsets("n2", h)), twin[t][:, half(h)], SUB)
+            else:
+                for h in range(2):
+                    nc.scalar.activation(diff[t][:, half(h)], d[t][:].indirect(offsets("n2", h)), COPY)
+                nc.vector.tensor_tensor(diff[t][:], diff[t][:], d[t][:], SUB)
+
+        def project(t):
+            y_acc = bank(t, "y_acc%d" % t, S)
             product(y_acc, w1, s13, 0, t, xw1[:], xs1[:])
             y[t] = sb("y%d" % t, [P, S], F32)
-            if t == 0:
+            if False:
                 nc.vector.tensor_scalar(y[t][:], y_acc[:], gain[:, t : t + 1], None, MULT)
             else:
                 nc.scalar.activation(y[t][:], y_acc[:], COPY, scale=gain[:, t : t + 1])
+
+        def squash(t):
             mix[t] = sb("mix%d" % t, [P, S], F32)
-            nc.scalar.activation(mix[t][:], diff[:], SIGMOID)
+            nc.scalar.activation(mix[t][:], diff[t][:], SIGMOID)
 
         def blend(t):
             u = sb("u%d" % t, [P, S], F32)
@@ -201,17 +212,29 @@ def tile_picked_triopullbgxbdet_none_po_kernel(
                 nc.scalar.activation(pulled[h][:, t, :], m[t][:].indirect(offsets("n4", h)), COPY, scale=-0.5)
             nc.vector.tensor_tensor(a[:, t, :], m[t][:], gate[t][:], MULT)
 
-        m = {}
-        front(0)
-        front(1)
-        front(2)
-        front(3)
-        gate_of(0, 0, nc.scalar.copy)
-        gate_of(1, 1, nc.scalar.copy)
+        m, d, twin, diff = {}, {}, {}, {}
+        spread(0)
+        spread(1)
+        spread(2)
+        spread(3)
+        differ(0)
+        differ(1)
+        differ(2)
+        differ(3)
+        project(0)
+        squash(0)
+        project(1)
+        squash(1)
+        project(2)
+        squash(2)
+        project(3)
+        squash(3)
+        gate_of(0, 4, nc.scalar.copy)
+        gate_of(1, 5, nc.scalar.copy)
         blend(0)
-        gate_of(2, 2, nc.scalar.copy)
+        gate_of(2, 6, nc.scalar.copy)
         blend(1)
-        gate_of(3, 3, nc.scalar.copy)
+        gate_of(3, 7, nc.scalar.copy)
         pull(0)
         blend(2)
         pull(1)
@@ -224,9 +247,9 @@ def tile_picked_triopullbgxbdet_none_po_kernel(
             h, w = c0 // HALF, c1 - c0
             z = keep.tile([P, w * PACK], BF16, name="z%d" % k, align_bytes=64)
             nc.vector.tensor_tensor(
-                z[:].rearrange("p (c i t) -> p c t i", t=PACK, i=4),
-                a[:, :, c0:c1].rearrange("p t (c i) -> p c t i", i=4),
-                pulled[h][:, :, c0 - h * HALF : c1 - h * HALF].rearrange("p t (c i) -> p c t i", i=4),
+                z[:].rearrange("p (c i t) -> p c t i", t=PACK, i=2),
+                a[:, :, c0:c1].rearrange("p t (c i) -> p c t i", i=2),
+                pulled[h][:, :, c0 - h * HALF : c1 - h * HALF].rearrange("p t (c i) -> p c t i", i=2),
                 ADD,
             )
             zw = sb("zw%d" % k, [P, w], U32)
@@ -235,7 +258,7 @@ def tile_picked_triopullbgxbdet_none_po_kernel(
             for t in range(PACK):
                 h_acc = bank((PACK * k + t) % 8, "h_acc%d_%d" % (k, t), w)
                 product(h_acc, w4, s4, 0, t, zw[:], zs[:])
-                if k == 3 and t % 2 == 1:
+                if k == 3 or (k == 2 and t >= 2):
                     nc.vector.tensor_copy(hs[t][:, c0:c1], h_acc[:])
                 else:
                     nc.scalar.copy(hs[t][:, c0:c1], h_acc[:])
@@ -250,10 +273,13 @@ def tile_picked_triopullbgxbdet_none_po_kernel(
                 terms = []
                 for first, second, factor in (("n5", "n6", 0.75), ("n7", "n8", -0.75)):
                     g = sb("g%s_%d_%d" % (first, t, k), [P, w], F32)
-                    nc.scalar.activation(g[:], hs[t][:].indirect(lists[first][:, c0 // 16 : c1 // 16]), COPY, scale=factor)
+                    if first == "n5" and t == 0 and k == 0:
+                        nc.vector.tensor_scalar(g[:], hs[t][:].indirect(lists[first][:, c0 // 16 : c1 // 16]), factor, 0.0, MULT, ADD)
+                    else:
+                        nc.scalar.activation(g[:], hs[t][:].indirect(lists[first][:, c0 // 16 : c1 // 16]), COPY, scale=factor)
                     term = sb("term%s_%d_%d" % (first, t, k), [P, w], F32)
                     window = hs[t][:].indirect(lists[second][:, c0 // 16 : c1 // 16])
-                    if first == "n7" and t == 2:
+                    if first == "n7" and (t == 2 or (t == 0 and k == 1)):
                         g2 = sb("gg%s_%d_%d" % (first, t, k), [P, w], F32)
                         nc.scalar.activation(g2[:], window, COPY)
                         nc.vector.tensor_tensor(term[:], g2[:], g[:], MULT)
@@ -267,10 +293,10 @@ def tile_picked_triopullbgxbdet_none_po_kernel(
                 nc.vector.tensor_tensor(o[:, t, :], terms[0][:], terms[1][:], ADD)
                 nc.sync.dma_start(out_rows[:, t, c0:c1], o[:, t, :])
             ob = sb("ob%d" % k, [P, w * PACK], BF16)
-            cast = nc.scalar.copy if k == 0 else nc.vector.tensor_copy
+            cast = nc.scalar.copy if False else nc.vector.tensor_copy
             cast(
-                ob[:].rearrange("p (c i t) -> p c t i", t=PACK, i=4),
-                o[:].rearrange("p t (c i) -> p c t i", i=4),
+                ob[:].rearrange("p (c i t) -> p c t i", t=PACK, i=2),
+                o[:].rearrange("p t (c i) -> p c t i", i=2),
             )
             ow = sb("ow%d" % k, [P, w], U32)
             nc.vector.quantize_mx(ow[:].bitcast(FP8X4), o_scales[:, c0:c1], ob[:])

@@ -145,6 +145,10 @@ def tile_picked_triopullbgxbdet_none_po_kernel(
                     bias=bias[:, t : t + 1], scale=slope[:, t : t + 1],
                 )
 
+        warm = sb("warm", [P, 1], F32)
+        nc.vector.memset(warm[:], 0.0)
+        warm_out = sb("warm_out", [P, 1], F32)
+        nc.scalar.activation(warm_out[:], warm[:], SIGMOID)
         xs2 = pick_scales("two")
         xs1 = pick_scales("offs")
         xw2 = pick_words("two", "pw_a")

@@ -19,8 +19,13 @@ P = 128
 T = 2048
 S = 512
 PACK = 4
+QUADRANTS = 4
+PER_COLUMN = 16
 HALF = S // 2
-FLOPS = 4 * 2 * 512 * 512 * 512
+QUARTER = S // 4
+BANKS = 8
+LINE = 16
+FLOPS = 4 * 2 * S * S * S
 
 
 def tile_picked_triopullbgxbdet_none_po_kernel(
@@ -31,6 +36,7 @@ def tile_picked_triopullbgxbdet_none_po_kernel(
     with ExitStack() as ctx:
         keep = ctx.enter_context(tc.tile_pool(name="keep", bufs=1))
         psum = ctx.enter_context(tc.psum_pool(name="psum", bufs=1))
+        lists = {}
 
         def sb(name, shape, dtype):
             return keep.tile(shape, dtype, name=name, align_bytes=64)
@@ -38,44 +44,35 @@ def tile_picked_triopullbgxbdet_none_po_kernel(
         def bank(number, name, width):
             return psum.tile([P, width], F32, name=name, tag="bank%d" % number)
 
-        lists = {}
+        def half(side):
+            return slice(side * HALF, (side + 1) * HALF)
+
+        def entries(name, cols):
+            return lists[name][:, cols.start // PER_COLUMN : cols.stop // PER_COLUMN]
 
         def load_list(name, ap):
-            lists[name] = sb("list_" + name, [P, S // 16], U16)
+            lists[name] = sb("list_" + name, [P, S // PER_COLUMN], U16)
             nc.sync.dma_start(lists[name][:], ap)
 
-        def offsets(name, h):
-            return lists[name][:, h * HALF // 16 : (h + 1) * HALF // 16]
-
-        def half(h):
-            return slice(h * HALF, (h + 1) * HALF)
-
-        def load_words(queue, name, ap, width):
+        def load_words(name, ap, width):
             words = sb(name, [P, width], U32)
-            queue.dma_start(words[:].bitcast(I32), ap[0].rearrange("p n t -> p (n t)").bitcast(I32))
+            nc.sync.dma_start(words[:].bitcast(I32), ap[0].rearrange("p n t -> p (n t)").bitcast(I32))
             return words
 
-        def load_scales(queue, name, ap, width):
-            plane = sb(name, [P, width], U8)
-            for q in range(4):
-                rows = ap[0, 4 * q : 4 * q + 4, :].bitcast(I32)
-                queue.dma_start(plane[32 * q : 32 * q + 32, :].bitcast(I32), rows.partition_broadcast(8))
-            return plane
-
         def zeroed_plane(name):
-            plane = keep.tile([P, S], U8, name=name, tag=name, align_bytes=64)
+            plane = sb(name, [P, S], U8)
             nc.vector.memset(plane[:].bitcast(I32), 0)
             return plane
 
-        def load_rows(plane, first, ap):
-            for q in range(4):
-                rows = slice(32 * q + first, 32 * q + first + 4)
-                nc.sync.dma_start(plane[rows, :].bitcast(I32), ap[0, 4 * q : 4 * q + 4, :].bitcast(I32))
+        def load_scale_rows(plane, first, ap):
+            for q in range(QUADRANTS):
+                live = slice(32 * q + first, 32 * q + first + 4)
+                nc.sync.dma_start(plane[live, :].bitcast(I32), ap[0, 4 * q : 4 * q + 4, :].bitcast(I32))
 
-        def load_column(queue, name, ap):
-            column = sb(name, [P, PACK], F32)
-            queue.dma_start(column[:], ap.rearrange("(p t) o -> p (t o)", t=PACK))
-            return column
+        def load_row_values(name, ap):
+            values = sb(name, [P, PACK], F32)
+            nc.sync.dma_start(values[:], ap.rearrange("(p t) o -> p (t o)", t=PACK))
+            return values
 
         def deal(copy, name, raw, dtype, run):
             dealt = sb(name, [P, S], dtype)
@@ -85,228 +82,197 @@ def tile_picked_triopullbgxbdet_none_po_kernel(
             )
             return dealt
 
-        raw_s13 = zeroed_plane("raw_s13")
-        raw_s2 = zeroed_plane("raw_s2")
-        raw_s4 = zeroed_plane("raw_s4")
-        load_list("two", two)
-        xs = load_scales(nc.sync, "xs", x_scales, T)
-        load_list("offs", offs)
-        xw = load_words(nc.sync, "xw", x_words, T)
-        load_rows(raw_s2, 0, w2_scales)
-        raw_w2 = load_words(nc.sync, "raw_w2", w2_words, S)
-        load_list("three", three)
-        raw_w3 = load_words(nc.sync, "raw_w3", w3_words, S)
-        load_rows(raw_s13, 0, w1_scales)
-        load_rows(raw_s13, 4, w3_scales)
-        raw_w1 = load_words(nc.sync, "raw_w1", w1_words, S)
-        gain = load_column(nc.sync, "gain", gn)
-        load_list("n2", n2)
-        slope = load_column(nc.sync, "slope", sl)
-        thresh = load_column(nc.sync, "thresh", th)
-        load_list("n3", n3)
-        load_list("n1", n1)
-        load_list("n4", n4)
-        raw_w4 = load_words(nc.sync, "raw_w4", w4_words, S)
-        load_rows(raw_s4, 0, w4_scales)
-        load_list("n5", n5)
-        load_list("n6", n6)
-        load_list("n7", n7)
-        load_list("n8", n8)
+        def deal_words(copy, name, raw):
+            return deal(copy, name, raw, U32, LINE // 4)
 
-        def pick_words(name, tag):
-            words = keep.tile([P, S], U32, name="pw_" + name, tag=tag, align_bytes=64)
-            nc.vector.tensor_copy(words[:], xw[:].indirect(lists[name][:]))
+        def deal_plane(copy, name, raw):
+            return deal(copy, name, raw, U8, LINE)
+
+        def pick_words(name, buffer):
+            words = keep.tile([P, S], U32, name="picked_words_" + name, tag=buffer, align_bytes=64)
+            nc.vector.tensor_copy(words[:], x_word_table[:].indirect(lists[name][:]))
             return words
 
         def pick_scales(name):
-            scales = sb("ps_" + name, [P, S], U8)
-            nc.vector.tensor_copy(scales[:], xs[:].indirect(lists[name][:]))
+            scales = sb("picked_scales_" + name, [P, S], U8)
+            nc.vector.tensor_copy(scales[:], x_scale_table[:].indirect(lists[name][:]))
             return scales
 
         def product(acc, w_words, w_plane, first, t, words, scales):
             cols = slice(t * P, (t + 1) * P)
             nc.tensor.matmul_mx(
                 out=acc[:], lhsT=w_words[:, cols].bitcast(FP8X4), lhsT_scale=w_plane[first:P, cols],
-                rhs=words.bitcast(FP8X4), rhs_scale=scales, start=True, stop=True,
+                rhs=words[:].bitcast(FP8X4), rhs_scale=scales[:], start=True, stop=True,
             )
 
-        bias = sb("bias", [P, PACK], F32)
-        gate = {}
+        def side_by_side(narrow):
+            return narrow.rearrange("p (c i t) -> p c t i", t=PACK, i=2)
 
-        def gate_of(t, number, copy):
-            acc = bank(number, "b_acc%d" % t, S)
-            product(acc, w3, s13, 4, t, xw3[:], xs3[:])
-            b = sb("b%d" % t, [P, S], F32)
-            copy(b[:], acc[:])
-            gate[t] = sb("sg%d" % t, [P, S], F32)
-            for h in range(2):
-                nc.scalar.activation(
-                    gate[t][:, half(h)], b[:].indirect(offsets("n3", h)), SIGMOID,
-                    bias=bias[:, t : t + 1], scale=slope[:, t : t + 1],
-                )
+        def by_tiles(values):
+            return values.rearrange("p t (c i) -> p c t i", i=2)
 
-        warm = sb("warm", [P, 1], F32)
-        nc.vector.memset(warm[:], 0.0)
+        raw_plane13 = zeroed_plane("raw_plane13")
+        raw_plane2 = zeroed_plane("raw_plane2")
+        raw_plane4 = zeroed_plane("raw_plane4")
+        load_list("two", two)
+        x_scale_table = sb("x_scale_table", [P, T], U8)
+        for q in range(QUADRANTS):
+            four_rows = x_scales[0, 4 * q : 4 * q + 4, :].bitcast(I32)
+            nc.sync.dma_start(x_scale_table[32 * q : 32 * q + 32, :].bitcast(I32), four_rows.partition_broadcast(8))
+        load_list("offs", offs)
+        x_word_table = load_words("x_word_table", x_words, T)
+        load_scale_rows(raw_plane2, 0, w2_scales)
+        raw_w2 = load_words("raw_w2", w2_words, S)
+        load_list("three", three)
+        raw_w3 = load_words("raw_w3", w3_words, S)
+        load_scale_rows(raw_plane13, 0, w1_scales)
+        load_scale_rows(raw_plane13, 4, w3_scales)
+        raw_w1 = load_words("raw_w1", w1_words, S)
+        load_list("n2", n2)
+        gain = load_row_values("gain", gn)
+
+        warm_in = sb("warm_in", [P, 1], F32)
+        nc.vector.memset(warm_in[:], 0.0)
         warm_out = sb("warm_out", [P, 1], F32)
-        nc.scalar.activation(warm_out[:], warm[:], SIGMOID)
-        xs2 = pick_scales("two")
-        xs1 = pick_scales("offs")
-        xw2 = pick_words("two", "pw_a")
-        s2 = deal(nc.vector.tensor_copy, "s2", raw_s2, U8, 16)
-        w2 = deal(nc.scalar.copy, "w2", raw_w2, U32, 4)
+        nc.scalar.activation(warm_out[:], warm_in[:], SIGMOID)
+
+        scales_two = pick_scales("two")
+        scales_idx = pick_scales("offs")
+        words_two = pick_words("two", "words_a")
+        plane2 = deal_plane(nc.gpsimd.tensor_copy, "plane2", raw_plane2)
+        w2 = deal_words(nc.scalar.copy, "w2", raw_w2)
         d_accs = [bank(t, "d_acc%d" % t, S) for t in range(PACK)]
         for t in range(PACK):
-            product(d_accs[t], w2, s2, 0, t, xw2[:], xs2[:])
-        xs3 = pick_scales("three")
-        xw3 = pick_words("three", "pw_b")
-        w3 = deal(nc.scalar.copy, "w3", raw_w3, U32, 4)
-        s13 = deal(nc.vector.tensor_copy, "s13", raw_s13, U8, 16)
+            product(d_accs[t], w2, plane2, 0, t, words_two, scales_two)
+
+        d, d_copy = [], []
+        for t in range(PACK):
+            d.append(sb("d%d" % t, [P, 2 * S], F32))
+            d_copy.append(sb("d_copy%d" % t, [P, S], F32))
+            for cols in [half(0), half(1)] if t == 0 else [slice(0, S)]:
+                nc.scalar.copy(d[t][:, cols], d_accs[t][:, cols])
+                nc.sync.dma_start(d_copy[t][:, cols], d[t][:, cols])
+
+        slope = load_row_values("slope", sl)
+        thresh = load_row_values("thresh", th)
+        for name, ap in (("n3", n3), ("n1", n1), ("n4", n4)):
+            load_list(name, ap)
+        raw_w4 = load_words("raw_w4", w4_words, S)
+        load_scale_rows(raw_plane4, 0, w4_scales)
+        for name, ap in (("n5", n5), ("n6", n6), ("n7", n7), ("n8", n8)):
+            load_list(name, ap)
+
+        scales_three = pick_scales("three")
+        words_three = pick_words("three", "words_b")
+        w3 = deal_words(nc.scalar.copy, "w3", raw_w3)
+        plane13 = deal_plane(nc.gpsimd.tensor_copy, "plane13", raw_plane13)
+        bias = sb("bias", [P, PACK], F32)
         nc.vector.scalar_tensor_tensor(bias[:], slope[:], -1.0, thresh[:], MULT, MULT)
-        xw1 = pick_words("offs", "raw_s13")
-        w1 = deal(nc.scalar.copy, "w1", raw_w1, U32, 4)
-        w4 = deal(nc.scalar.copy, "w4", raw_w4, U32, 4)
-        s4 = deal(nc.vector.tensor_copy, "s4", raw_s4, U8, 16)
+        words_idx = pick_words("offs", "words_a")
+        w1 = deal_words(nc.gpsimd.tensor_copy, "w1", raw_w1)
+        w4 = deal_words(nc.scalar.copy, "w4", raw_w4)
+        plane4 = deal_plane(nc.vector.tensor_copy, "plane4", raw_plane4)
 
-        mix = {}
-        y = {}
-        a = sb("a", [P, PACK, S], F32)
-        pulled = [sb("pulled%d" % h, [P, PACK, HALF], F32) for h in range(2)]
+        diff = []
+        for t in range(PACK):
+            diff.append(sb("diff%d" % t, [P, S], F32))
+            for cols in [half(0), half(1)] if t == 0 else [slice(0, S)]:
+                nc.vector.tensor_tensor(diff[t][:, cols], d[t][:].indirect(entries("n2", cols)), d_copy[t][:, cols], SUB)
 
-        def spread(t):
-            d[t] = sb("d%d" % t, [P, S], F32)
-            nc.scalar.copy(d[t][:], d_accs[t][:])
-            if True:
-                twin[t] = sb("twin%d" % t, [P, S], F32)
-                nc.scalar.dma_start(twin[t][:], d[t][:])
-
-        def differ(t):
-            diff[t] = sb("diff%d" % t, [P, S], F32)
-            if True:
-                for h in range(2):
-                    nc.vector.tensor_tensor(diff[t][:, half(h)], d[t][:].indirect(offsets("n2", h)), twin[t][:, half(h)], SUB)
-            else:
-                for h in range(2):
-                    nc.scalar.activation(diff[t][:, half(h)], d[t][:].indirect(offsets("n2", h)), COPY)
-                nc.vector.tensor_tensor(diff[t][:], diff[t][:], d[t][:], SUB)
-
-        def project(t):
+        gy, mix = [], []
+        for t in range(PACK):
             y_acc = bank(t, "y_acc%d" % t, S)
-            product(y_acc, w1, s13, 0, t, xw1[:], xs1[:])
-            y[t] = sb("y%d" % t, [P, S], F32)
-            if False:
-                nc.vector.tensor_scalar(y[t][:], y_acc[:], gain[:, t : t + 1], None, MULT)
-            else:
-                nc.scalar.activation(y[t][:], y_acc[:], COPY, scale=gain[:, t : t + 1])
-
-        def squash(t):
-            mix[t] = sb("mix%d" % t, [P, S], F32)
+            product(y_acc, w1, plane13, 0, t, words_idx, scales_idx)
+            gy.append(sb("gy%d" % t, [P, 2 * S], F32))
+            nc.scalar.activation(gy[t][:, :S], y_acc[:], COPY, scale=gain[:, t : t + 1])
+            mix.append(sb("mix%d" % t, [P, S], F32))
             nc.scalar.activation(mix[t][:], diff[t][:], SIGMOID)
 
+        sg, gm = [], []
+        gated = sb("gated", [P, PACK, S], F32)
+        pulled = [sb("pulled%d" % side, [P, PACK, HALF], F32) for side in range(2)]
+
+        def gate(t):
+            b_acc = bank(PACK + t, "b_acc%d" % t, S)
+            product(b_acc, w3, plane13, 4, t, words_three, scales_three)
+            b = sb("b%d" % t, [P, 2 * S], F32)
+            nc.scalar.copy(b[:, :S], b_acc[:])
+            sg.append(sb("sg%d" % t, [P, S], F32))
+            nc.scalar.activation(
+                sg[t][:], b[:].indirect(lists["n3"][:]), SIGMOID, bias=bias[:, t : t + 1], scale=slope[:, t : t + 1]
+            )
+
         def blend(t):
-            u = sb("u%d" % t, [P, S], F32)
-            for h in range(2):
-                nc.vector.tensor_tensor(u[:, half(h)], y[t][:].indirect(offsets("n1", h)), mix[t][:, half(h)], MULT)
-            v = sb("v%d" % t, [P, S], F32)
-            nc.vector.scalar_tensor_tensor(v[:], mix[t][:], 1.0, y[t][:], SUB, MULT)
-            m[t] = sb("m%d" % t, [P, S], F32)
-            nc.vector.tensor_tensor(m[t][:], u[:], v[:], SUB)
+            fetched = sb("fetched%d" % t, [P, S], F32)
+            nc.vector.tensor_tensor(fetched[:], gy[t][:].indirect(lists["n1"][:]), mix[t][:], MULT)
+            own = sb("own%d" % t, [P, S], F32)
+            nc.vector.scalar_tensor_tensor(own[:], mix[t][:], 1.0, gy[t][:, :S], SUB, MULT)
+            gm.append(sb("gm%d" % t, [P, S], F32))
+            nc.vector.tensor_tensor(gm[t][:], fetched[:], own[:], SUB)
 
         def pull(t):
-            for h in range(2):
-                nc.scalar.activation(pulled[h][:, t, :], m[t][:].indirect(offsets("n4", h)), COPY, scale=-0.5)
-            nc.vector.tensor_tensor(a[:, t, :], m[t][:], gate[t][:], MULT)
+            for side in range(2):
+                looked_up = gm[t][:].indirect(entries("n4", half(side)))
+                nc.scalar.activation(pulled[side][:, t, :], looked_up, COPY, scale=-0.5)
+            nc.vector.tensor_tensor(gated[:, t, :], gm[t][:], sg[t][:], MULT)
 
-        m, d, twin, diff = {}, {}, {}, {}
-        spread(0)
-        spread(1)
-        spread(2)
-        spread(3)
-        differ(0)
-        differ(1)
-        differ(2)
-        differ(3)
-        project(0)
-        squash(0)
-        project(1)
-        squash(1)
-        project(2)
-        squash(2)
-        project(3)
-        squash(3)
-        gate_of(0, 4, nc.scalar.copy)
-        gate_of(1, 5, nc.scalar.copy)
-        blend(0)
-        gate_of(2, 6, nc.scalar.copy)
-        blend(1)
-        gate_of(3, 7, nc.scalar.copy)
-        pull(0)
-        blend(2)
-        pull(1)
-        blend(3)
-        pull(2)
-        pull(3)
+        for step in range(PACK + 3):
+            for stage, lag in ((gate, 0), (pull, 3), (blend, 1)):
+                if 0 <= step - lag < PACK:
+                    stage(step - lag)
 
-        hs = [sb("h%d" % t, [P, S], F32) for t in range(PACK)]
-        for k, (c0, c1) in enumerate(((0,128),(128,256),(256,384),(384,512))):
-            h, w = c0 // HALF, c1 - c0
-            z = keep.tile([P, w * PACK], BF16, name="z%d" % k, align_bytes=64)
+        h_rows = [sb("h%d" % t, [P, S], F32) for t in range(PACK)]
+        for k in range(S // QUARTER):
+            cols = slice(k * QUARTER, (k + 1) * QUARTER)
+            within = slice(cols.start % HALF, cols.start % HALF + QUARTER)
+            z = sb("z%d" % k, [P, QUARTER * PACK], BF16)
             nc.vector.tensor_tensor(
-                z[:].rearrange("p (c i t) -> p c t i", t=PACK, i=2),
-                a[:, :, c0:c1].rearrange("p t (c i) -> p c t i", i=2),
-                pulled[h][:, :, c0 - h * HALF : c1 - h * HALF].rearrange("p t (c i) -> p c t i", i=2),
-                ADD,
+                side_by_side(z[:]), by_tiles(gated[:, :, cols]), by_tiles(pulled[cols.start // HALF][:, :, within]), ADD
             )
-            zw = sb("zw%d" % k, [P, w], U32)
-            zs = sb("zs%d" % k, [P, w], U8)
-            nc.vector.quantize_mx(zw[:].bitcast(FP8X4), zs[:], z[:])
+            z_words = sb("z_words%d" % k, [P, QUARTER], U32)
+            z_plane = sb("z_plane%d" % k, [P, QUARTER], U8)
+            nc.vector.quantize_mx(z_words[:].bitcast(FP8X4), z_plane[:], z[:])
+            copy_out = nc.vector.tensor_copy if cols.stop == S else nc.scalar.copy
             for t in range(PACK):
-                h_acc = bank((PACK * k + t) % 8, "h_acc%d_%d" % (k, t), w)
-                product(h_acc, w4, s4, 0, t, zw[:], zs[:])
-                if k == 3 or (k == 2 and t >= 2):
-                    nc.vector.tensor_copy(hs[t][:, c0:c1], h_acc[:])
-                else:
-                    nc.scalar.copy(hs[t][:, c0:c1], h_acc[:])
+                h_acc = bank((PACK * k + t) % BANKS, "h_acc%d_%d" % (k, t), QUARTER)
+                product(h_acc, w4, plane4, 0, t, z_words, z_plane)
+                copy_out(h_rows[t][:, cols], h_acc[:])
 
         out_rows = out_0.rearrange("(p t) n -> p t n", t=PACK)
         out_words = out_1[0].rearrange("p n t -> p (n t)").bitcast(I32)
-        o_scales = sb("o_scales", [P, S], U8)
-        for k, (c0, c1) in enumerate(((0,256),(256,512))):
-            w = c1 - c0
-            o = sb("o%d" % k, [P, PACK, w], F32)
+        out_plane = sb("out_plane", [P, S], U8)
+        for side in range(2):
+            cols = half(side)
+            result = sb("result%d" % side, [P, PACK, HALF], F32)
             for t in range(PACK):
                 terms = []
-                for first, second, factor in (("n5", "n6", 0.75), ("n7", "n8", -0.75)):
-                    g = sb("g%s_%d_%d" % (first, t, k), [P, w], F32)
-                    if first == "n5" and t == 0 and k == 0:
-                        nc.vector.tensor_scalar(g[:], hs[t][:].indirect(lists[first][:, c0 // 16 : c1 // 16]), factor, 0.0, MULT, ADD)
+                for j, (left_list, right_list, factor) in enumerate((("n5", "n6", 0.75), ("n7", "n8", -0.75))):
+                    label = "%d_%d_%d" % (side, t, j)
+                    left = sb("left" + label, [P, HALF], F32)
+                    left_of_h = h_rows[t][:].indirect(entries(left_list, cols))
+                    if side == 0 and t == 0 and j == 0:
+                        nc.vector.tensor_scalar(left[:], left_of_h, factor, 0.0, MULT, ADD)
                     else:
-                        nc.scalar.activation(g[:], hs[t][:].indirect(lists[first][:, c0 // 16 : c1 // 16]), COPY, scale=factor)
-                    term = sb("term%s_%d_%d" % (first, t, k), [P, w], F32)
-                    window = hs[t][:].indirect(lists[second][:, c0 // 16 : c1 // 16])
-                    if first == "n7" and (t == 2 or (t == 0 and k == 1)):
-                        g2 = sb("gg%s_%d_%d" % (first, t, k), [P, w], F32)
-                        nc.scalar.activation(g2[:], window, COPY)
-                        nc.vector.tensor_tensor(term[:], g2[:], g[:], MULT)
-                    elif False:
-                        g2 = sb("gg%s_%d_%d" % (first, t, k), [P, w], F32)
-                        nc.vector.tensor_copy(g2[:], window)
-                        nc.vector.tensor_tensor(term[:], g2[:], g[:], MULT)
+                        nc.scalar.activation(left[:], left_of_h, COPY, scale=factor)
+                    term = sb("term" + label, [P, HALF], F32)
+                    right_of_h = h_rows[t][:].indirect(entries(right_list, cols))
+                    if side == 1 and j == 1:
+                        right = sb("right" + label, [P, HALF], F32)
+                        nc.scalar.activation(right[:], right_of_h, COPY)
+                        nc.vector.tensor_tensor(term[:], right[:], left[:], MULT)
                     else:
-                        nc.vector.tensor_tensor(term[:], window, g[:], MULT)
+                        nc.vector.tensor_tensor(term[:], right_of_h, left[:], MULT)
                     terms.append(term)
-                nc.vector.tensor_tensor(o[:, t, :], terms[0][:], terms[1][:], ADD)
-                nc.sync.dma_start(out_rows[:, t, c0:c1], o[:, t, :])
-            ob = sb("ob%d" % k, [P, w * PACK], BF16)
-            cast = nc.scalar.copy if False else nc.vector.tensor_copy
-            cast(
-                ob[:].rearrange("p (c i t) -> p c t i", t=PACK, i=2),
-                o[:].rearrange("p t (c i) -> p c t i", i=2),
-            )
-            ow = sb("ow%d" % k, [P, w], U32)
-            nc.vector.quantize_mx(ow[:].bitcast(FP8X4), o_scales[:, c0:c1], ob[:])
-            nc.sync.dma_start(out_words[:, c0:c1], ow[:].bitcast(I32))
-        for q in range(4):
+                nc.vector.tensor_tensor(result[:, t, :], terms[0][:], terms[1][:], ADD)
+                nc.sync.dma_start(out_rows[:, t, cols], result[:, t, :])
+            rounded = sb("rounded%d" % side, [P, HALF * PACK], BF16)
+            nc.vector.tensor_copy(side_by_side(rounded[:]), by_tiles(result[:]))
+            codes = sb("codes%d" % side, [P, HALF], U32)
+            nc.vector.quantize_mx(codes[:].bitcast(FP8X4), out_plane[:, cols], rounded[:])
+            nc.sync.dma_start(out_words[:, cols], codes[:].bitcast(I32))
+
+        for q in range(QUADRANTS):
             queue = nc.sync if q % 2 == 0 else nc.scalar
             queue.dma_start(
-                out_2[0, 4 * q : 4 * q + 4, :].bitcast(I32), o_scales[32 * q : 32 * q + 4, :].bitcast(I32)
+                out_2[0, 4 * q : 4 * q + 4, :].bitcast(I32), out_plane[32 * q : 32 * q + 4, :].bitcast(I32)
             )

from contextlib import ExitStack

import concourse.mybir as mybir

F32 = mybir.dt.float32
BF16 = mybir.dt.bfloat16
I32 = mybir.dt.int32
U32 = mybir.dt.uint32
U16 = mybir.dt.uint16
U8 = mybir.dt.uint8
FP8X4 = mybir.dt.float8_e4m3fn_x4
MULT = mybir.AluOpType.mult
ADD = mybir.AluOpType.add
SUB = mybir.AluOpType.subtract
COPY = mybir.ActivationFunctionType.Copy
SIGMOID = mybir.ActivationFunctionType.Sigmoid

P = 128
T = 2048
S = 512
PACK = 4
QUADRANTS = 4
PER_COLUMN = 16
HALF = S // 2
QUARTER = S // 4
BANKS = 8
LINE = 16
FLOPS = 4 * 2 * S * S * S


def tile_picked_triopullbgxbdet_none_po_kernel(
    tc, x_words, x_scales, w1_words, w1_scales, w2_words, w2_scales, w3_words, w3_scales, sl, th, gn,
    w4_words, w4_scales, offs, two, three, n1, n2, n3, n4, n5, n6, n7, n8, out_0, out_1, out_2,
):
    nc = tc.nc
    with ExitStack() as ctx:
        keep = ctx.enter_context(tc.tile_pool(name="keep", bufs=1))
        psum = ctx.enter_context(tc.psum_pool(name="psum", bufs=1))
        lists = {}

        def sb(name, shape, dtype):
            return keep.tile(shape, dtype, name=name, align_bytes=64)

        def bank(number, name, width):
            return psum.tile([P, width], F32, name=name, tag="bank%d" % number)

        def half(side):
            return slice(side * HALF, (side + 1) * HALF)

        def entries(name, cols):
            return lists[name][:, cols.start // PER_COLUMN : cols.stop // PER_COLUMN]

        def load_list(name, ap):
            lists[name] = sb("list_" + name, [P, S // PER_COLUMN], U16)
            nc.sync.dma_start(lists[name][:], ap)

        def load_words(name, ap, width):
            words = sb(name, [P, width], U32)
            nc.sync.dma_start(words[:].bitcast(I32), ap[0].rearrange("p n t -> p (n t)").bitcast(I32))
            return words

        def zeroed_plane(name):
            plane = sb(name, [P, S], U8)
            nc.vector.memset(plane[:].bitcast(I32), 0)
            return plane

        def load_scale_rows(plane, first, ap):
            for q in range(QUADRANTS):
                live = slice(32 * q + first, 32 * q + first + 4)
                nc.sync.dma_start(plane[live, :].bitcast(I32), ap[0, 4 * q : 4 * q + 4, :].bitcast(I32))

        def load_row_values(name, ap):
            values = sb(name, [P, PACK], F32)
            nc.sync.dma_start(values[:], ap.rearrange("(p t) o -> p (t o)", t=PACK))
            return values

        def deal(copy, name, raw, dtype, run):
            dealt = sb(name, [P, S], dtype)
            copy(
                dealt[:].rearrange("p (t c i) -> p c t i", t=PACK, i=run),
                raw[:].rearrange("p (c i t) -> p c t i", t=PACK, i=run),
            )
            return dealt

        def deal_words(copy, name, raw):
            return deal(copy, name, raw, U32, LINE // 4)

        def deal_plane(copy, name, raw):
            return deal(copy, name, raw, U8, LINE)

        def pick_words(name, buffer):
            words = keep.tile([P, S], U32, name="picked_words_" + name, tag=buffer, align_bytes=64)
            nc.vector.tensor_copy(words[:], x_word_table[:].indirect(lists[name][:]))
            return words

        def pick_scales(name):
            scales = sb("picked_scales_" + name, [P, S], U8)
            nc.vector.tensor_copy(scales[:], x_scale_table[:].indirect(lists[name][:]))
            return scales

        def product(acc, w_words, w_plane, first, t, words, scales):
            cols = slice(t * P, (t + 1) * P)
            nc.tensor.matmul_mx(
                out=acc[:], lhsT=w_words[:, cols].bitcast(FP8X4), lhsT_scale=w_plane[first:P, cols],
                rhs=words[:].bitcast(FP8X4), rhs_scale=scales[:], start=True, stop=True,
            )

        def side_by_side(narrow):
            return narrow.rearrange("p (c i t) -> p c t i", t=PACK, i=2)

        def by_tiles(values):
            return values.rearrange("p t (c i) -> p c t i", i=2)

        raw_plane13 = zeroed_plane("raw_plane13")
        raw_plane2 = zeroed_plane("raw_plane2")
        raw_plane4 = zeroed_plane("raw_plane4")
        load_list("two", two)
        x_scale_table = sb("x_scale_table", [P, T], U8)
        for q in range(QUADRANTS):
            four_rows = x_scales[0, 4 * q : 4 * q + 4, :].bitcast(I32)
            nc.sync.dma_start(x_scale_table[32 * q : 32 * q + 32, :].bitcast(I32), four_rows.partition_broadcast(8))
        load_list("offs", offs)
        x_word_table = load_words("x_word_table", x_words, T)
        load_scale_rows(raw_plane2, 0, w2_scales)
        raw_w2 = load_words("raw_w2", w2_words, S)
        load_list("three", three)
        raw_w3 = load_words("raw_w3", w3_words, S)
        load_scale_rows(raw_plane13, 0, w1_scales)
        load_scale_rows(raw_plane13, 4, w3_scales)
        raw_w1 = load_words("raw_w1", w1_words, S)
        load_list("n2", n2)
        gain = load_row_values("gain", gn)

        warm_in = sb("warm_in", [P, 1], F32)
        nc.vector.memset(warm_in[:], 0.0)
        warm_out = sb("warm_out", [P, 1], F32)
        nc.scalar.activation(warm_out[:], warm_in[:], SIGMOID)

        scales_two = pick_scales("two")
        scales_idx = pick_scales("offs")
        words_two = pick_words("two", "words_a")
        plane2 = deal_plane(nc.gpsimd.tensor_copy, "plane2", raw_plane2)
        w2 = deal_words(nc.scalar.copy, "w2", raw_w2)
        d_accs = [bank(t, "d_acc%d" % t, S) for t in range(PACK)]
        for t in range(PACK):
            product(d_accs[t], w2, plane2, 0, t, words_two, scales_two)

        d, d_copy = [], []
        for t in range(PACK):
            d.append(sb("d%d" % t, [P, 2 * S], F32))
            d_copy.append(sb("d_copy%d" % t, [P, S], F32))
            for cols in [half(0), half(1)] if t == 0 else [slice(0, S)]:
                nc.scalar.copy(d[t][:, cols], d_accs[t][:, cols])
                nc.sync.dma_start(d_copy[t][:, cols], d[t][:, cols])

        slope = load_row_values("slope", sl)
        thresh = load_row_values("thresh", th)
        for name, ap in (("n3", n3), ("n1", n1), ("n4", n4)):
            load_list(name, ap)
        raw_w4 = load_words("raw_w4", w4_words, S)
        load_scale_rows(raw_plane4, 0, w4_scales)
        for name, ap in (("n5", n5), ("n6", n6), ("n7", n7), ("n8", n8)):
            load_list(name, ap)

        scales_three = pick_scales("three")
        words_three = pick_words("three", "words_b")
        w3 = deal_words(nc.scalar.copy, "w3", raw_w3)
        plane13 = deal_plane(nc.gpsimd.tensor_copy, "plane13", raw_plane13)
        bias = sb("bias", [P, PACK], F32)
        nc.vector.scalar_tensor_tensor(bias[:], slope[:], -1.0, thresh[:], MULT, MULT)
        words_idx = pick_words("offs", "words_a")
        w1 = deal_words(nc.gpsimd.tensor_copy, "w1", raw_w1)
        w4 = deal_words(nc.scalar.copy, "w4", raw_w4)
        plane4 = deal_plane(nc.vector.tensor_copy, "plane4", raw_plane4)

        diff = []
        for t in range(PACK):
            diff.append(sb("diff%d" % t, [P, S], F32))
            for cols in [half(0), half(1)] if t == 0 else [slice(0, S)]:
                nc.vector.tensor_tensor(diff[t][:, cols], d[t][:].indirect(entries("n2", cols)), d_copy[t][:, cols], SUB)

        gy, mix = [], []
        for t in range(PACK):
            y_acc = bank(t, "y_acc%d" % t, S)
            product(y_acc, w1, plane13, 0, t, words_idx, scales_idx)
            gy.append(sb("gy%d" % t, [P, 2 * S], F32))
            nc.scalar.activation(gy[t][:, :S], y_acc[:], COPY, scale=gain[:, t : t + 1])
            mix.append(sb("mix%d" % t, [P, S], F32))
            nc.scalar.activation(mix[t][:], diff[t][:], SIGMOID)

        sg, gm = [], []
        gated = sb("gated", [P, PACK, S], F32)
        pulled = [sb("pulled%d" % side, [P, PACK, HALF], F32) for side in range(2)]

        def gate(t):
            b_acc = bank(PACK + t, "b_acc%d" % t, S)
            product(b_acc, w3, plane13, 4, t, words_three, scales_three)
            b = sb("b%d" % t, [P, 2 * S], F32)
            nc.scalar.copy(b[:, :S], b_acc[:])
            sg.append(sb("sg%d" % t, [P, S], F32))
            nc.scalar.activation(
                sg[t][:], b[:].indirect(lists["n3"][:]), SIGMOID, bias=bias[:, t : t + 1], scale=slope[:, t : t + 1]
            )

        def blend(t):
            fetched = sb("fetched%d" % t, [P, S], F32)
            nc.vector.tensor_tensor(fetched[:], gy[t][:].indirect(lists["n1"][:]), mix[t][:], MULT)
            own = sb("own%d" % t, [P, S], F32)
            nc.vector.scalar_tensor_tensor(own[:], mix[t][:], 1.0, gy[t][:, :S], SUB, MULT)
            gm.append(sb("gm%d" % t, [P, S], F32))
            nc.vector.tensor_tensor(gm[t][:], fetched[:], own[:], SUB)

        def pull(t):
            for side in range(2):
                looked_up = gm[t][:].indirect(entries("n4", half(side)))
                nc.scalar.activation(pulled[side][:, t, :], looked_up, COPY, scale=-0.5)
            nc.vector.tensor_tensor(gated[:, t, :], gm[t][:], sg[t][:], MULT)

        for step in range(PACK + 3):
            for stage, lag in ((gate, 0), (pull, 3), (blend, 1)):
                if 0 <= step - lag < PACK:
                    stage(step - lag)

        h_rows = [sb("h%d" % t, [P, S], F32) for t in range(PACK)]
        for k in range(S // QUARTER):
            cols = slice(k * QUARTER, (k + 1) * QUARTER)
            within = slice(cols.start % HALF, cols.start % HALF + QUARTER)
            z = sb("z%d" % k, [P, QUARTER * PACK], BF16)
            nc.vector.tensor_tensor(
                side_by_side(z[:]), by_tiles(gated[:, :, cols]), by_tiles(pulled[cols.start // HALF][:, :, within]), ADD
            )
            z_words = sb("z_words%d" % k, [P, QUARTER], U32)
            z_plane = sb("z_plane%d" % k, [P, QUARTER], U8)
            nc.vector.quantize_mx(z_words[:].bitcast(FP8X4), z_plane[:], z[:])
            copy_out = nc.vector.tensor_copy if cols.stop == S else nc.scalar.copy
            for t in range(PACK):
                h_acc = bank((PACK * k + t) % BANKS, "h_acc%d_%d" % (k, t), QUARTER)
                product(h_acc, w4, plane4, 0, t, z_words, z_plane)
                copy_out(h_rows[t][:, cols], h_acc[:])

        out_rows = out_0.rearrange("(p t) n -> p t n", t=PACK)
        out_words = out_1[0].rearrange("p n t -> p (n t)").bitcast(I32)
        out_plane = sb("out_plane", [P, S], U8)
        for side in range(2):
            cols = half(side)
            result = sb("result%d" % side, [P, PACK, HALF], F32)
            for t in range(PACK):
                terms = []
                for j, (left_list, right_list, factor) in enumerate((("n5", "n6", 0.75), ("n7", "n8", -0.75))):
                    label = "%d_%d_%d" % (side, t, j)
                    left = sb("left" + label, [P, HALF], F32)
                    left_of_h = h_rows[t][:].indirect(entries(left_list, cols))
                    if side == 0 and t == 0 and j == 0:
                        nc.vector.tensor_scalar(left[:], left_of_h, factor, 0.0, MULT, ADD)
                    else:
                        nc.scalar.activation(left[:], left_of_h, COPY, scale=factor)
                    term = sb("term" + label, [P, HALF], F32)
                    right_of_h = h_rows[t][:].indirect(entries(right_list, cols))
                    if side == 1 and j == 1:
                        right = sb("right" + label, [P, HALF], F32)
                        nc.scalar.activation(right[:], right_of_h, COPY)
                        nc.vector.tensor_tensor(term[:], right[:], left[:], MULT)
                    else:
                        nc.vector.tensor_tensor(term[:], right_of_h, left[:], MULT)
                    terms.append(term)
                nc.vector.tensor_tensor(result[:, t, :], terms[0][:], terms[1][:], ADD)
                nc.sync.dma_start(out_rows[:, t, cols], result[:, t, :])
            rounded = sb("rounded%d" % side, [P, HALF * PACK], BF16)
            nc.vector.tensor_copy(side_by_side(rounded[:]), by_tiles(result[:]))
            codes = sb("codes%d" % side, [P, HALF], U32)
            nc.vector.quantize_mx(codes[:].bitcast(FP8X4), out_plane[:, cols], rounded[:])
            nc.sync.dma_start(out_words[:, cols], codes[:].bitcast(I32))

        for q in range(QUADRANTS):
            queue = nc.sync if q % 2 == 0 else nc.scalar
            queue.dma_start(
                out_2[0, 4 * q : 4 * q + 4, :].bitcast(I32), out_plane[32 * q : 32 * q + 4, :].bitcast(I32)
            )
